import numpy as np
import ml_dtypes


def mxq(x, axis, fmt="e4m3"):
    dtype, down = {"e4m3": (ml_dtypes.float8_e4m3fn, 7), "e5m2": (ml_dtypes.float8_e5m2, 14)}[fmt]
    v = np.moveaxis(np.asarray(x, np.float32).astype(ml_dtypes.bfloat16).astype(np.float64), axis, -1)
    blocks = v.reshape(v.shape[:-1] + (-1, 32))
    amax = np.abs(blocks).max(-1, keepdims=True)
    byte = np.maximum(np.where(amax > 0, np.frexp(amax)[1] - 1 + 127, 0) - down, 1)
    scale = np.exp2(byte - 127.0)
    codes = (blocks / scale).astype(np.float32).astype(dtype).astype(np.float64)
    return np.moveaxis((codes * scale).reshape(v.shape), -1, axis)


WIDE = False


def mx_kscale(k, group=512):
    if not WIDE:
        return np.ones(k)
    levels = np.array([10, -10, 5, -5, 0])
    if group != 512:
        return np.exp2(np.random.permutation(np.resize(levels, k // group))).repeat(group)
    if k % 512:
        return np.exp2(np.random.permutation(np.resize(levels, k // 32))).repeat(32)
    a = np.empty((k // 512, 16))
    for p in range(k // 512):
        a[p, :8] = np.random.permutation(np.resize(levels, 8))
        for g in range(8):
            far = levels[np.abs(levels - a[p, g]) >= 10]
            a[p, g + 8] = far[np.random.randint(len(far))]
    return np.exp2(a.ravel()).repeat(32)


def f64(x):
    return np.asarray(x).astype(np.float64)


def striped(idx):
    return np.tile(np.asarray(idx).reshape(-1, 16).T, (8, 1)).astype(np.uint16)


def unstriped(offs):
    return offs[:16].T.reshape(-1).astype(np.int64)


H, KV, D, NQ, N = 4, 2, 256, 512, 512
CAP = 2.0


def setup_inputs():
    n = np.random.standard_normal
    s = mx_kscale(D, 0)[:, None]
    u = mx_kscale(N)
    t = np.random.uniform(0.5, 2.0, N) * u
    v = n((KV, N, 128))
    return {
        "qT": (n((H, D, NQ)) * s * (0.70 / np.sqrt(D))).astype(np.float32),
        "kT": (n((KV, D, N)) / s).astype(np.float32),
        "t": t.reshape(N, 1).astype(np.float32),
        "v": (v / t[:, None]).astype(np.float32),
        "kb": (0.5 * n((N, 1))).astype(np.float32),
        "mask": (np.arange(N)[:, None] <= np.sort(np.random.randint(N // 4, N, NQ))[None, :]).astype(np.float32),
    }


def reference(qT, kT, t, v, kb, mask):
    a = np.repeat(mxq(f64(kT), 1, "e4m3"), H // KV, 0).transpose(0, 2, 1) @ mxq(f64(qT), 1, "e4m3")
    a = a + f64(kb)
    a = CAP * np.tanh(a / CAP)
    p = 1.0 / (1.0 + np.exp(-a))
    p = p * f64(mask)
    w = p * f64(t)
    y = mxq(w, 1, "e4m3").transpose(0, 2, 1) @ np.repeat(mxq(f64(v), 1, "e4m3"), H // KV, 0)
    y = y / 16.0
    return y

@@ -1,0 +1,351 @@
+from contextlib import ExitStack
+
+import concourse.mybir as mybir
+
+H, KV, D, NQ, N, E = 4, 2, 256, 512, 512, 128
+FLOPS = 2 * H * N * NQ * D + 2 * H * NQ * N * E
+
+F32 = mybir.dt.float32
+BF16 = mybir.dt.bfloat16
+U32 = mybir.dt.uint32
+U8 = mybir.dt.uint8
+FP8X4 = mybir.dt.float8_e4m3fn_x4
+ACT = mybir.ActivationFunctionType
+ALU = mybir.AluOpType
+
+P = 128
+ROWS = 64
+PACK = 4
+MM = 128
+BANK = 512
+
+UNITS = [
+    (0, 0, 0, 128), (0, 1, 0, 128), (0, 0, 128, 384), (0, 1, 128, 384),
+    (1, 0, 0, 512), (1, 1, 0, 256), (1, 1, 256, 128), (1, 1, 384, 128),
+]
+PLACE = [
+    [(0, 0), (1, 0), (2, 0), (2, 128)],
+    [(0, 0), (1, 0), (2, 0), (2, 128)],
+    [(0, 0), (1, 0), (2, 0), (0, 0)],
+    [(0, 0), (1, 0), (2, 0), (0, 0)],
+    [(1, 0), (2, 0), (0, 0), (1, 0)],
+    [(1, 0), (1, 256), (2, 0), (2, 256)],
+    [(0, 0), (0, 128), (0, 256), (0, 384)],
+    [(1, 0), (1, 128), (1, 256), (1, 384)],
+]
+Y_PLACE = [(0, 0), (1, 0), (0, 128), (1, 128), (0, 0), (1, 0), (1, 256), (0, 0)]
+HEAD = [[1, 2], [0, 3]]
+
+
+def tile_rows_a_sigmoid_kb_mask_cap_kernel(tc, qT, kT, t, v, kb, mask, out):
+    nc = tc.nc
+    with ExitStack() as ctx:
+        sb = ctx.enter_context(tc.tile_pool(name="sb", bufs=1))
+        ps = ctx.enter_context(tc.psum_pool(name="ps", bufs=1))
+        ctx.enter_context(tc.manual_schedule())
+
+        def tile(name, shape, dtype):
+            return sb.tile(shape, dtype, name=name, align_bytes=64)
+
+        score_banks = [[ps.tile([P, BANK], F32, name="score%d_%d" % (g, b)) for b in range(3)] for g in range(2)]
+        y_banks = [ps.tile([P, BANK], F32, name="y%d" % b) for b in range(2)]
+
+        k_raw = tile("k_raw", [P, PACK, N], F32)
+        kb_sb = tile("kb_sb", [P, PACK], F32)
+        t_sb = tile("t_sb", [P, PACK], F32)
+        v_raw = tile("v_raw", [P, KV, PACK, E], F32)
+        q_rows = qT.rearrange("h d n -> (h d) n")
+        q_raw = {}
+        mask_raw = {}
+
+        def load_q(pair, q0, w):
+            raw = tile("q_raw%d_%d" % (pair, q0), [P, PACK, w], F32)
+            q_raw[(pair, q0)] = raw
+            if pair == 0:
+                nc.sync.dma_start(out=raw[:], in_=q_rows[D : 3 * D, q0 : q0 + w].rearrange("(p j) n -> p j n", j=PACK))
+            else:
+                for g in range(2):
+                    nc.sync.dma_start(
+                        out=raw[ROWS * g : ROWS * (g + 1)],
+                        in_=qT[HEAD[pair][g], :, q0 : q0 + w].rearrange("(p j) n -> p j n", j=PACK),
+                    )
+
+        def load_mask(q0, w):
+            raw = tile("mask_raw%d" % q0, [P, PACK, w], F32)
+            mask_raw[q0] = raw
+            nc.sync.dma_start(out=raw[:], in_=mask[:, q0 : q0 + w].rearrange("(p j) n -> p j n", j=PACK))
+
+        nc.scalar.dma_start(out=kb_sb[:], in_=kb.rearrange("(p j) o -> p (j o)", j=PACK))
+        nc.scalar.dma_start(out=t_sb[:], in_=t.rearrange("(p j) o -> p (j o)", j=PACK))
+        nc.sync.dma_start(out=k_raw[:], in_=kT.rearrange("h (p j) n -> (h p) j n", j=PACK))
+        load_q(0, 0, 128)
+        load_q(0, 128, 384)
+        load_mask(0, 128)
+        nc.sync.dma_start(out=v_raw[:], in_=v.rearrange("h (p j) e -> p h j e", j=PACK))
+        load_mask(128, 384)
+        load_q(1, 0, 256)
+        load_q(1, 256, 256)
+
+        kb_half = tile("kb_half", [P, PACK], F32)
+        nc.gpsimd.tensor_scalar(out=kb_half[:], in0=kb_sb[:], scalar1=0.5, scalar2=0.0, op0=ALU.mult, op1=ALU.add)
+
+        def interleave(eng_copy, dst, src):
+            eng_copy(out=dst.rearrange("p (c i) j -> p c j i", i=2), in_=src.rearrange("p j (c i) -> p c j i", i=2))
+
+        def quantize(codes, scales, src):
+            nc.vector.quantize_mx(out=codes.bitcast(FP8X4), scales=scales, in_=src)
+
+        k_bf = [tile("k_bf%d" % u, [P, 2, MM, PACK], BF16) for u in range(2)]
+        k_codes = [tile("k_codes%d" % u, [P, 2 * MM], U32) for u in range(2)]
+        k_scales = [tile("k_scales%d" % u, [P, 2 * MM], U8) for u in range(2)]
+
+        def cast_k(copy, u):
+            copy(
+                out=k_bf[u][:].rearrange("p i s j -> p s j i"),
+                in_=k_raw[:].rearrange("p j (s u i) -> p u s j i", u=2, i=2)[:, u],
+            )
+
+        def quant_k(u):
+            quantize(k_codes[u][:], k_scales[u][:], k_bf[u][:].rearrange("p i s j -> p (i s j)"))
+
+        q_bf = [tile("q_bf%d" % a, [P, NQ, PACK], BF16) for a in range(2)]
+        q_codes = [tile("q_codes%d" % a, [P, NQ], U32) for a in range(2)]
+        q_scales = [tile("q_scales%d" % a, [P, NQ], U8) for a in range(2)]
+
+        def cast_q(pair, q0, w):
+            interleave(nc.vector.tensor_copy, q_bf[pair][:, q0 : q0 + w, :], q_raw[(pair, q0)][:])
+
+        def quant_q(pair, q0, w):
+            quantize(
+                q_codes[pair][:, q0 : q0 + w],
+                q_scales[pair][:, q0 : q0 + w],
+                q_bf[pair][:, q0 : q0 + w, :].rearrange("p n j -> p (n j)"),
+            )
+
+        v_bf = tile("v_bf", [P, KV, E, PACK], BF16)
+        v_codes = tile("v_codes", [P, KV * E], U32)
+        v_scales = tile("v_scales", [P, KV * E], U8)
+
+        def cast_v():
+            for g in range(KV):
+                interleave(nc.vector.tensor_copy, v_bf[:, g], v_raw[:, g])
+
+        def quant_v():
+            quantize(v_codes[:], v_scales[:], v_bf[:].rearrange("p h e j -> p (h e j)"))
+
+        mt = tile("mt", [P, PACK, NQ], F32)
+
+        def scale_mask(q0, w):
+            for r in range(PACK):
+                nc.vector.tensor_scalar(
+                    out=mt[:, r, q0 : q0 + w], in0=mask_raw[q0][:, r, :], scalar1=t_sb[:, r : r + 1], scalar2=None, op0=ALU.mult
+                )
+
+        capped = [tile("capped%d" % n, [P, PACK, u[3]], F32) for n, u in enumerate(UNITS)]
+        prob = [tile("prob%d" % n, [P, PACK, u[3]], F32) for n, u in enumerate(UNITS)]
+        w_bf = [tile("w_bf%d" % n, [P, u[3], PACK], BF16) for n, u in enumerate(UNITS)]
+        w_codes = [tile("w_codes%d" % n, [P, u[3]], U32) for n, u in enumerate(UNITS)]
+        w_scales = [tile("w_scales%d" % n, [P, u[3]], U8) for n, u in enumerate(UNITS)]
+        y_sb = [tile("y_sb%d" % h, [P, NQ // MM, E], F32) for h in range(H)]
+
+        place = {(n, r): (score_banks[UNITS[n][1]][b], c) for n in range(len(UNITS)) for r, (b, c) in enumerate(PLACE[n])}
+
+        def scores(n, r):
+            pair, g, q0, w = UNITS[n]
+            bank, c0 = place[(n, r)]
+            rows = slice(ROWS * g, ROWS * (g + 1))
+            kc = slice((r % 2) * MM, (r % 2 + 1) * MM)
+            for c in range(0, w, MM):
+                qc = slice(q0 + c, q0 + c + MM)
+                nc.tensor.matmul_mx(
+                    out=bank[:, c0 + c : c0 + c + MM],
+                    lhsT=k_codes[r // 2][rows, kc].bitcast(FP8X4),
+                    lhsT_scale=k_scales[r // 2][rows, kc],
+                    rhs=q_codes[pair][rows, qc].bitcast(FP8X4),
+                    rhs_scale=q_scales[pair][rows, qc],
+                    start=True,
+                    stop=True,
+                )
+
+        def cap(n, r):
+            w = UNITS[n][3]
+            bank, c0 = place[(n, r)]
+            nc.scalar.activation(
+                out=capped[n][:, r, :], in_=bank[:, c0 : c0 + w], func=ACT.Tanh, bias=kb_half[:, r : r + 1], scale=0.5
+            )
+
+        def sigmoid(n, c0, w, r0=0, r1=PACK):
+            nc.scalar.activation(
+                out=prob[n][:, r0:r1, c0 : c0 + w], in_=capped[n][:, r0:r1, c0 : c0 + w], func=ACT.Sigmoid, scale=2.0
+            )
+
+        def weigh(n, c0, w):
+            q0 = UNITS[n][2] + c0
+            nc.vector.tensor_tensor(
+                out=w_bf[n][:, c0 : c0 + w, :].rearrange("p (c i) r -> p c r i", i=2),
+                in0=prob[n][:, :, c0 : c0 + w].rearrange("p r (c i) -> p c r i", i=2),
+                in1=mt[:, :, q0 : q0 + w].rearrange("p r (c i) -> p c r i", i=2),
+                op=ALU.mult,
+            )
+
+        def quant_w(n, c0, w):
+            quantize(
+                w_codes[n][:, c0 : c0 + w],
+                w_scales[n][:, c0 : c0 + w],
+                w_bf[n][:, c0 : c0 + w, :].rearrange("p n r -> p (n r)"),
+            )
+
+        def values(n, c0, w):
+            g = UNITS[n][1]
+            vc = slice(g * E, (g + 1) * E)
+            for c in range(c0, c0 + w, MM):
+                nc.tensor.matmul_mx(
+                    out=y_banks[Y_PLACE[n][0]][:, Y_PLACE[n][1] + c : Y_PLACE[n][1] + c + E],
+                    lhsT=w_codes[n][:, c : c + MM].bitcast(FP8X4),
+                    lhsT_scale=w_scales[n][:, c : c + MM],
+                    rhs=v_codes[:, vc].bitcast(FP8X4),
+                    rhs_scale=v_scales[:, vc],
+                    start=True,
+                    stop=True,
+                )
+
+        def finish(h, q0, w, bank, c0, on_scalar=False):
+            blocks = slice(q0 // MM, (q0 + w) // MM)
+            dst = y_sb[h][:, blocks, :].rearrange("p c e -> p (c e)")
+            src = y_banks[bank][:, c0 : c0 + w]
+            if on_scalar:
+                nc.scalar.activation(out=dst, in_=src, func=ACT.Copy, scale=1.0 / 16.0)
+            else:
+                nc.vector.tensor_scalar(out=dst, in0=src, scalar1=1.0 / 16.0, scalar2=None, op0=ALU.mult)
+            nc.sync.dma_start(out=out[h, q0 : q0 + w, :].rearrange("(c m) e -> m c e", m=MM), in_=y_sb[h][:, blocks, :])
+
+        cast_k(nc.vector.tensor_copy, 0)
+        cast_k(nc.scalar.copy, 1)
+        cast_q(0, 0, 128)
+        quant_k(0)
+        quant_q(0, 0, 128)
+        quant_k(1)
+        scores(0,0)
+        scores(1,0)
+        scores(0,1)
+        scores(1,1)
+        scores(0,2)
+        scores(0,3)
+        scores(1,2)
+        scores(1,3)
+        cap(0,0)
+        cap(1,0)
+        cap(0,1)
+        cap(1,1)
+        cap(0,2)
+        cap(0,3)
+        cap(1,2)
+        cap(1,3)
+        cast_q(0,128,384)
+        scale_mask(0,128)
+        quant_q(0,128,128)
+        quant_q(0,256,256)
+        sigmoid(0,0,128)
+        sigmoid(1,0,128)
+        scores(2,0)
+        scores(2,1)
+        scores(2,2)
+        scores(3,0)
+        cast_v()
+        weigh(0,0,128)
+        quant_v()
+        weigh(1,0,128)
+        quant_w(0,0,128)
+        cap(2,0)
+        cap(2,1)
+        scores(2,3)
+        scores(3,1)
+        cap(2,2)
+        cap(3,0)
+        cap(2,3)
+        scores(3,2)
+        scores(3,3)
+        cap(3,1)
+        scale_mask(128,384)
+        quant_w(1,0,128)
+        cast_q(1,0,256)
+        values(0,0,128)
+        values(1,0,128)
+        sigmoid(2,0,128)
+        sigmoid(2,128,256)
+        cast_q(1,256,256)
+        quant_q(1,0,256)
+        weigh(2,0,128)
+        quant_q(1,256,256)
+        scores(4,0)
+        scores(4,1)
+        scores(4,2)
+        weigh(2,128,256)
+        quant_w(2,0,128)
+        cap(3,2)
+        cap(3,3)
+        cap(4,0)
+        sigmoid(3,0,128)
+        sigmoid(3,128,256)
+        scores(4,3)
+        scores(5,0)
+        scores(5,1)
+        scores(5,2)
+        scores(5,3)
+        weigh(3,0,128)
+        quant_w(2,128,256)
+        values(2,0,384)
+        weigh(3,128,256)
+        quant_w(3,0,128)
+        finish(1,0,512,0,0)
+        quant_w(3,128,256)
+        cap(4,1)
+        cap(4,2)
+        cap(4,3)
+        cap(5,0)
+        sigmoid(4,0,256)
+        sigmoid(4,256,256)
+        scores(6,0)
+        scores(6,1)
+        scores(6,2)
+        scores(6,3)
+        values(3,0,384)
+        weigh(4,0,256)
+        finish(2,0,512,1,0)
+        weigh(4,256,256)
+        quant_w(4,0,256)
+        cap(5,1)
+        scores(7,0)
+        scores(7,1)
+        scores(7,2)
+        scores(7,3)
+        cap(5,2)
+        cap(5,3)
+        cap(6,0)
+        sigmoid(5,0,256)
+        quant_w(4,256,256)
+        values(4,0,512)
+        weigh(5,0,256)
+        cap(6,1)
+        cap(6,2)
+        cap(6,3)
+        cap(7,0)
+        sigmoid(6,0,128)
+        quant_w(5,0,256)
+        values(5,0,256)
+        weigh(6,0,128)
+        cap(7,1)
+        cap(7,2)
+        cap(7,3)
+        sigmoid(7,0,64)
+        sigmoid(7,64,64)
+        quant_w(6,0,128)
+        values(6,0,128)
+        weigh(7,0,64)
+        weigh(7,64,64)
+        quant_w(7,0,64)
+        quant_w(7,64,64)
+        finish(0,0,512,0,0,True)
+        finish(3,0,384,1,0,True)
+        values(7,0,128)
+        finish(3,384,128,0,0,True)

@@ -19,21 +19,9 @@ PACK = 4
 MM = 128
 BANK = 512
 
-UNITS = [
-    (0, 0, 0, 128), (0, 1, 0, 128), (0, 0, 128, 384), (0, 1, 128, 384),
-    (1, 0, 0, 512), (1, 1, 0, 256), (1, 1, 256, 128), (1, 1, 384, 128),
-]
-PLACE = [
-    [(0, 0), (1, 0), (2, 0), (2, 128)],
-    [(0, 0), (1, 0), (2, 0), (2, 128)],
-    [(0, 0), (1, 0), (2, 0), (0, 0)],
-    [(0, 0), (1, 0), (2, 0), (0, 0)],
-    [(1, 0), (2, 0), (0, 0), (1, 0)],
-    [(1, 0), (1, 256), (2, 0), (2, 256)],
-    [(0, 0), (0, 128), (0, 256), (0, 384)],
-    [(1, 0), (1, 128), (1, 256), (1, 384)],
-]
-Y_PLACE = [(0, 0), (1, 0), (0, 128), (1, 128), (0, 0), (1, 0), (1, 256), (0, 0)]
+UNITS = [[0,0,0,128],[0,1,0,128],[0,0,128,384],[0,1,128,384],[1,0,0,256],[1,1,0,256],[1,0,256,256],[1,1,256,128],[1,1,384,128]]
+PLACE = [[[0,0],[1,0],[2,0],[2,128]],[[0,0],[1,0],[2,0],[2,128]],[[0,0],[1,0],[2,0],[0,0]],[[0,0],[1,0],[2,0],[0,0]],[[1,0],[1,256],[2,0],[2,256]],[[1,0],[1,256],[2,0],[2,256]],[[0,0],[0,256],[1,0],[1,256]],[[0,0],[0,128],[0,256],[0,384]],[[1,0],[1,128],[1,256],[1,384]]]
+Y_PLACE = [(0, 0), (1, 0), (0, 128), (1, 128), (0, 0), (1, 0), (0, 256), (1, 256), (0, 0)]
 HEAD = [[1, 2], [0, 3]]
 
 
@@ -55,39 +43,40 @@ def tile_rows_a_sigmoid_kb_mask_cap_kernel(tc, qT, kT, t, v, kb, mask, out):
         t_sb = tile("t_sb", [P, PACK], F32)
         v_raw = tile("v_raw", [P, KV, PACK, E], F32)
         q_rows = qT.rearrange("h d n -> (h d) n")
-        q_raw = {}
-        mask_raw = {}
+        q_raw = [tile("q_raw%d" % a, [P, PACK, NQ], F32) for a in range(2)]
+        mask_raw = tile("mask_raw", [P, PACK, NQ], F32)
 
-        def load_q(pair, q0, w):
-            raw = tile("q_raw%d_%d" % (pair, q0), [P, PACK, w], F32)
-            q_raw[(pair, q0)] = raw
-            if pair == 0:
-                nc.sync.dma_start(out=raw[:], in_=q_rows[D : 3 * D, q0 : q0 + w].rearrange("(p j) n -> p j n", j=PACK))
-            else:
-                for g in range(2):
-                    nc.sync.dma_start(
-                        out=raw[ROWS * g : ROWS * (g + 1)],
-                        in_=qT[HEAD[pair][g], :, q0 : q0 + w].rearrange("(p j) n -> p j n", j=PACK),
-                    )
+        def load_q0(q0, w):
+            nc.sync.dma_start(
+                out=q_raw[0][:, :, q0 : q0 + w], in_=q_rows[D : 3 * D, q0 : q0 + w].rearrange("(p j) n -> p j n", j=PACK)
+            )
 
-        def load_mask(q0, w):
-            raw = tile("mask_raw%d" % q0, [P, PACK, w], F32)
-            mask_raw[q0] = raw
-            nc.sync.dma_start(out=raw[:], in_=mask[:, q0 : q0 + w].rearrange("(p j) n -> p j n", j=PACK))
+        def load_q1(queue, g):
+            queue.dma_start(
+                out=q_raw[1][ROWS * g : ROWS * (g + 1)], in_=qT[HEAD[1][g]].rearrange("(p j) n -> p j n", j=PACK)
+            )
 
         nc.scalar.dma_start(out=kb_sb[:], in_=kb.rearrange("(p j) o -> p (j o)", j=PACK))
         nc.scalar.dma_start(out=t_sb[:], in_=t.rearrange("(p j) o -> p (j o)", j=PACK))
         nc.sync.dma_start(out=k_raw[:], in_=kT.rearrange("h (p j) n -> (h p) j n", j=PACK))
-        load_q(0, 0, 128)
-        load_q(0, 128, 384)
-        load_mask(0, 128)
+        load_q0(0, 128)
+        load_q0(128, 384)
+        nc.sync.dma_start(out=mask_raw[:], in_=mask.rearrange("(p j) n -> p j n", j=PACK))
+        load_q1(nc.sync, 0)
         nc.sync.dma_start(out=v_raw[:], in_=v.rearrange("h (p j) e -> p h j e", j=PACK))
-        load_mask(128, 384)
-        load_q(1, 0, 256)
-        load_q(1, 256, 256)
+
+        warm = tile("warm", [P, 8], F32)
+        warm_out = tile("warm_out", [P, 8], F32)
+        nc.vector.memset(warm[:], 0.0)
+        nc.scalar.activation(out=warm_out[:], in_=warm[:], func=ACT.Sigmoid)
 
         kb_half = tile("kb_half", [P, PACK], F32)
-        nc.gpsimd.tensor_scalar(out=kb_half[:], in0=kb_sb[:], scalar1=0.5, scalar2=0.0, op0=ALU.mult, op1=ALU.add)
+
+        def halve_kb():
+            nc.vector.tensor_scalar(out=kb_half[:], in0=kb_sb[:], scalar1=0.5, scalar2=None, op0=ALU.mult)
+
+        def load_h3():
+            load_q1(nc.scalar, 1)
 
         def interleave(eng_copy, dst, src):
             eng_copy(out=dst.rearrange("p (c i) j -> p c j i", i=2), in_=src.rearrange("p j (c i) -> p c j i", i=2))
@@ -113,7 +102,7 @@ def tile_rows_a_sigmoid_kb_mask_cap_kernel(tc, qT, kT, t, v, kb, mask, out):
         q_scales = [tile("q_scales%d" % a, [P, NQ], U8) for a in range(2)]
 
         def cast_q(pair, q0, w):
-            interleave(nc.vector.tensor_copy, q_bf[pair][:, q0 : q0 + w, :], q_raw[(pair, q0)][:])
+            interleave(nc.vector.tensor_copy, q_bf[pair][:, q0 : q0 + w, :], q_raw[pair][:, :, q0 : q0 + w])
 
         def quant_q(pair, q0, w):
             quantize(
@@ -126,9 +115,8 @@ def tile_rows_a_sigmoid_kb_mask_cap_kernel(tc, qT, kT, t, v, kb, mask, out):
         v_codes = tile("v_codes", [P, KV * E], U32)
         v_scales = tile("v_scales", [P, KV * E], U8)
 
-        def cast_v():
-            for g in range(KV):
-                interleave(nc.vector.tensor_copy, v_bf[:, g], v_raw[:, g])
+        def cast_v(g):
+            interleave(nc.vector.tensor_copy, v_bf[:, g], v_raw[:, g])
 
         def quant_v():
             quantize(v_codes[:], v_scales[:], v_bf[:].rearrange("p h e j -> p (h e j)"))
@@ -138,7 +126,7 @@ def tile_rows_a_sigmoid_kb_mask_cap_kernel(tc, qT, kT, t, v, kb, mask, out):
         def scale_mask(q0, w):
             for r in range(PACK):
                 nc.vector.tensor_scalar(
-                    out=mt[:, r, q0 : q0 + w], in0=mask_raw[q0][:, r, :], scalar1=t_sb[:, r : r + 1], scalar2=None, op0=ALU.mult
+                    out=mt[:, r, q0 : q0 + w], in0=mask_raw[:, r, q0 : q0 + w], scalar1=t_sb[:, r : r + 1], scalar2=None, op0=ALU.mult
                 )
 
         capped = [tile("capped%d" % n, [P, PACK, u[3]], F32) for n, u in enumerate(UNITS)]
@@ -150,12 +138,17 @@ def tile_rows_a_sigmoid_kb_mask_cap_kernel(tc, qT, kT, t, v, kb, mask, out):
 
         place = {(n, r): (score_banks[UNITS[n][1]][b], c) for n in range(len(UNITS)) for r, (b, c) in enumerate(PLACE[n])}
 
-        def scores(n, r):
+        def scores2(n, r):
+            for c in range(0, UNITS[n][3], MM):
+                scores(n, r, c)
+                scores(n + 1, r, c)
+
+        def scores(n, r, only=None):
             pair, g, q0, w = UNITS[n]
             bank, c0 = place[(n, r)]
             rows = slice(ROWS * g, ROWS * (g + 1))
             kc = slice((r % 2) * MM, (r % 2 + 1) * MM)
-            for c in range(0, w, MM):
+            for c in (range(0, w, MM) if only is None else [only]):
                 qc = slice(q0 + c, q0 + c + MM)
                 nc.tensor.matmul_mx(
                     out=bank[:, c0 + c : c0 + c + MM],
@@ -219,6 +212,7 @@ def tile_rows_a_sigmoid_kb_mask_cap_kernel(tc, qT, kT, t, v, kb, mask, out):
                 nc.vector.tensor_scalar(out=dst, in0=src, scalar1=1.0 / 16.0, scalar2=None, op0=ALU.mult)
             nc.sync.dma_start(out=out[h, q0 : q0 + w, :].rearrange("(c m) e -> m c e", m=MM), in_=y_sb[h][:, blocks, :])
 
+        halve_kb()
         cast_k(nc.vector.tensor_copy, 0)
         cast_k(nc.scalar.copy, 1)
         cast_q(0, 0, 128)
@@ -237,115 +231,120 @@ def tile_rows_a_sigmoid_kb_mask_cap_kernel(tc, qT, kT, t, v, kb, mask, out):
         cap(1,0)
         cap(0,1)
         cap(1,1)
+        load_h3()
         cap(0,2)
         cap(0,3)
         cap(1,2)
         cap(1,3)
-        cast_q(0,128,384)
-        scale_mask(0,128)
+        cast_q(0,128,128)
+        cast_q(0,256,256)
         quant_q(0,128,128)
         quant_q(0,256,256)
+        scale_mask(0,512)
         sigmoid(0,0,128)
         sigmoid(1,0,128)
-        scores(2,0)
-        scores(2,1)
-        scores(2,2)
-        scores(3,0)
-        cast_v()
+        scores2(2,0)
+        scores2(2,1)
+        scores2(2,2)
         weigh(0,0,128)
-        quant_v()
         weigh(1,0,128)
         quant_w(0,0,128)
-        cap(2,0)
-        cap(2,1)
-        scores(2,3)
-        scores(3,1)
-        cap(2,2)
-        cap(3,0)
-        cap(2,3)
-        scores(3,2)
-        scores(3,3)
-        cap(3,1)
-        scale_mask(128,384)
         quant_w(1,0,128)
+        cap(2,0)
+        cap(3,0)
+        scores2(2,3)
+        cap(2,1)
+        cap(3,1)
+        cap(2,2)
+        cap(3,2)
+        cap(2,3)
+        cap(3,3)
         cast_q(1,0,256)
-        values(0,0,128)
-        values(1,0,128)
+        cast_v(0)
+        quant_q(1,0,256)
+        cast_v(1)
+        cast_q(1,256,256)
+        quant_v()
+        quant_q(1,256,256)
         sigmoid(2,0,128)
         sigmoid(2,128,256)
-        cast_q(1,256,256)
-        quant_q(1,0,256)
-        weigh(2,0,128)
-        quant_q(1,256,256)
-        scores(4,0)
-        scores(4,1)
-        scores(4,2)
-        weigh(2,128,256)
-        quant_w(2,0,128)
-        cap(3,2)
-        cap(3,3)
-        cap(4,0)
         sigmoid(3,0,128)
-        sigmoid(3,128,256)
-        scores(4,3)
-        scores(5,0)
-        scores(5,1)
-        scores(5,2)
-        scores(5,3)
-        weigh(3,0,128)
-        quant_w(2,128,256)
-        values(2,0,384)
-        weigh(3,128,256)
-        quant_w(3,0,128)
-        finish(1,0,512,0,0)
-        quant_w(3,128,256)
-        cap(4,1)
-        cap(4,2)
-        cap(4,3)
-        cap(5,0)
-        sigmoid(4,0,256)
-        sigmoid(4,256,256)
+        scores2(4,0)
+        scores2(4,1)
+        scores2(4,2)
+        scores2(4,3)
         scores(6,0)
         scores(6,1)
-        scores(6,2)
-        scores(6,3)
-        values(3,0,384)
-        weigh(4,0,256)
-        finish(2,0,512,1,0)
-        weigh(4,256,256)
-        quant_w(4,0,256)
-        cap(5,1)
         scores(7,0)
         scores(7,1)
         scores(7,2)
         scores(7,3)
+        weigh(2,0,128)
+        weigh(2,128,256)
+        quant_w(2,0,128)
+        weigh(3,0,128)
+        quant_w(2,128,256)
+        cap(4,0)
+        cap(4,1)
+        sigmoid(3,128,256)
+        scores(6,2)
+        scores(6,3)
+        values(0,0,128)
+        values(2,0,384)
+        values(1,0,128)
+        weigh(3,128,256)
+        quant_w(3,0,128)
+        finish(1,0,512,0,0)
+        quant_w(3,128,256)
+        values(3,0,384)
+        cap(4,2)
+        cap(4,3)
+        cap(5,0)
+        cap(5,1)
+        sigmoid(4,0,256)
+        scores(8,0)
+        scores(8,1)
+        scores(8,2)
+        scores(8,3)
+        weigh(4,0,256)
+        finish(2,0,512,1,0)
+        quant_w(4,0,256)
+        values(4,0,256)
         cap(5,2)
         cap(5,3)
         cap(6,0)
         sigmoid(5,0,256)
-        quant_w(4,256,256)
-        values(4,0,512)
         weigh(5,0,256)
+        quant_w(5,0,256)
+        values(5,0,256)
         cap(6,1)
         cap(6,2)
         cap(6,3)
         cap(7,0)
-        sigmoid(6,0,128)
-        quant_w(5,0,256)
-        values(5,0,256)
-        weigh(6,0,128)
         cap(7,1)
+        sigmoid(6,0,256)
+        weigh(6,0,256)
+        quant_w(6,0,256)
+        values(6,0,256)
         cap(7,2)
         cap(7,3)
+        cap(8,0)
+        cap(8,1)
         sigmoid(7,0,64)
+        cap(8,2)
+        cap(8,3)
         sigmoid(7,64,64)
-        quant_w(6,0,128)
-        values(6,0,128)
+        sigmoid(8,0,64)
+        sigmoid(8,64,64)
         weigh(7,0,64)
         weigh(7,64,64)
-        quant_w(7,0,64)
-        quant_w(7,64,64)
+        weigh(8,0,64)
+        weigh(8,64,64)
+        quant_w(7,0,128)
+        quant_w(8,0,128)
+        finish(3,0,256,1,0,True)
         finish(0,0,512,0,0,True)
-        finish(3,0,384,1,0,True)
         values(7,0,128)
+        values(8,0,128)
+        finish(3,256,128,1,256)
         finish(3,384,128,0,0,True)

@@ -43,17 +43,17 @@ def tile_rows_a_sigmoid_kb_mask_cap_kernel(tc, qT, kT, t, v, kb, mask, out):
         t_sb = tile("t_sb", [P, PACK], F32)
         v_raw = tile("v_raw", [P, KV, PACK, E], F32)
         q_rows = qT.rearrange("h d n -> (h d) n")
-        q_raw = [tile("q_raw%d" % a, [P, PACK, NQ], F32) for a in range(2)]
+        q_raw = {(0, 0): tile("q_raw_a", [P, PACK, 128], F32), (0, 128): tile("q_raw_b", [P, PACK, 384], F32), (1, 0): tile("q_raw_c", [P, PACK, NQ], F32)}
         mask_raw = tile("mask_raw", [P, PACK, NQ], F32)
 
         def load_q0(q0, w):
             nc.sync.dma_start(
-                out=q_raw[0][:, :, q0 : q0 + w], in_=q_rows[D : 3 * D, q0 : q0 + w].rearrange("(p j) n -> p j n", j=PACK)
+                out=q_raw[(0, q0)][:], in_=q_rows[D : 3 * D, q0 : q0 + w].rearrange("(p j) n -> p j n", j=PACK)
             )
 
         def load_q1(queue, g):
             queue.dma_start(
-                out=q_raw[1][ROWS * g : ROWS * (g + 1)], in_=qT[HEAD[1][g]].rearrange("(p j) n -> p j n", j=PACK)
+                out=q_raw[(1, 0)][ROWS * g : ROWS * (g + 1)], in_=qT[HEAD[1][g]].rearrange("(p j) n -> p j n", j=PACK)
             )
 
         nc.scalar.dma_start(out=kb_sb[:], in_=kb.rearrange("(p j) o -> p (j o)", j=PACK))
@@ -102,7 +102,8 @@ def tile_rows_a_sigmoid_kb_mask_cap_kernel(tc, qT, kT, t, v, kb, mask, out):
         q_scales = [tile("q_scales%d" % a, [P, NQ], U8) for a in range(2)]
 
         def cast_q(pair, q0, w):
-            interleave(nc.vector.tensor_copy, q_bf[pair][:, q0 : q0 + w, :], q_raw[pair][:, :, q0 : q0 + w])
+            first = 128 if pair == 0 and q0 >= 128 else 0
+            interleave(nc.vector.tensor_copy, q_bf[pair][:, q0 : q0 + w, :], q_raw[(pair, first)][:, :, q0 - first : q0 - first + w])
 
         def quant_q(pair, q0, w):
             quantize(
@@ -130,7 +131,7 @@ def tile_rows_a_sigmoid_kb_mask_cap_kernel(tc, qT, kT, t, v, kb, mask, out):
                 )
 
         capped = [tile("capped%d" % n, [P, PACK, u[3]], F32) for n, u in enumerate(UNITS)]
-        prob = [tile("prob%d" % n, [P, PACK, u[3]], F32) for n, u in enumerate(UNITS)]
+        prob = {}
         w_bf = [tile("w_bf%d" % n, [P, u[3], PACK], BF16) for n, u in enumerate(UNITS)]
         w_codes = [tile("w_codes%d" % n, [P, u[3]], U32) for n, u in enumerate(UNITS)]
         w_scales = [tile("w_scales%d" % n, [P, u[3]], U8) for n, u in enumerate(UNITS)]
@@ -167,16 +168,15 @@ def tile_rows_a_sigmoid_kb_mask_cap_kernel(tc, qT, kT, t, v, kb, mask, out):
                 out=capped[n][:, r, :], in_=bank[:, c0 : c0 + w], func=ACT.Tanh, bias=kb_half[:, r : r + 1], scale=0.5
             )
 
-        def sigmoid(n, c0, w, r0=0, r1=PACK):
-            nc.scalar.activation(
-                out=prob[n][:, r0:r1, c0 : c0 + w], in_=capped[n][:, r0:r1, c0 : c0 + w], func=ACT.Sigmoid, scale=2.0
-            )
+        def sigmoid(n, c0, w):
+            prob[(n, c0)] = tile("prob%d_%d" % (n, c0), [P, PACK, w], F32)
+            nc.scalar.activation(out=prob[(n, c0)][:], in_=capped[n][:, :, c0 : c0 + w], func=ACT.Sigmoid, scale=2.0)
 
         def weigh(n, c0, w):
             q0 = UNITS[n][2] + c0
             nc.vector.tensor_tensor(
                 out=w_bf[n][:, c0 : c0 + w, :].rearrange("p (c i) r -> p c r i", i=2),
-                in0=prob[n][:, :, c0 : c0 + w].rearrange("p r (c i) -> p c r i", i=2),
+                in0=prob[(n, c0)][:].rearrange("p r (c i) -> p c r i", i=2),
                 in1=mt[:, :, q0 : q0 + w].rearrange("p r (c i) -> p c r i", i=2),
                 op=ALU.mult,
             )

@@ -40,7 +40,7 @@ def tile_rows_a_sigmoid_kb_mask_cap_kernel(tc, qT, kT, t, v, kb, mask, out):
 
         k_raw = tile("k_raw", [P, PACK, N], F32)
         kb_sb = tile("kb_sb", [P, PACK], F32)
-        t_sb = tile("t_sb", [P, PACK], F32)
+        t_sb = tile("t_sb", [P, 2, 1, 2], F32)
         v_raw = tile("v_raw", [P, KV, PACK, E], F32)
         q_rows = qT.rearrange("h d n -> (h d) n")
         q_raw = {(0, 0): tile("q_raw_a", [P, PACK, 128], F32), (0, 128): tile("q_raw_b", [P, PACK, 384], F32), (1, 0): tile("q_raw_c", [P, PACK, NQ], F32)}
@@ -57,11 +57,14 @@ def tile_rows_a_sigmoid_kb_mask_cap_kernel(tc, qT, kT, t, v, kb, mask, out):
             )
 
         nc.scalar.dma_start(out=kb_sb[:], in_=kb.rearrange("(p j) o -> p (j o)", j=PACK))
-        nc.scalar.dma_start(out=t_sb[:], in_=t.rearrange("(p j) o -> p (j o)", j=PACK))
+        nc.scalar.dma_start(out=t_sb[:].rearrange("p u o l -> p (u o l)"), in_=t.rearrange("(p j) o -> p (j o)", j=PACK))
         nc.sync.dma_start(out=k_raw[:], in_=kT.rearrange("h (p j) n -> (h p) j n", j=PACK))
         load_q0(0, 128)
         load_q0(128, 384)
-        nc.sync.dma_start(out=mask_raw[:], in_=mask.rearrange("(p j) n -> p j n", j=PACK))
+        for u in range(2):
+            nc.sync.dma_start(
+                out=mask_raw[:, 2 * u : 2 * u + 2, :], in_=mask.rearrange("(p j) n -> p j n", j=PACK)[:, 2 * u : 2 * u + 2, :]
+            )
         load_q1(nc.sync, 0)
         nc.sync.dma_start(out=v_raw[:], in_=v.rearrange("h (p j) e -> p h j e", j=PACK))
 
@@ -90,8 +93,8 @@ def tile_rows_a_sigmoid_kb_mask_cap_kernel(tc, qT, kT, t, v, kb, mask, out):
 
         def cast_k(copy, u):
             copy(
-                out=k_bf[u][:].rearrange("p i s j -> p s j i"),
-                in_=k_raw[:].rearrange("p j (s u i) -> p u s j i", u=2, i=2)[:, u],
+                out=k_bf[u][:].rearrange("p i s j -> p s i j"),
+                in_=k_raw[:].rearrange("p j (s u i) -> p u s i j", u=2, i=2)[:, u],
             )
 
         def quant_k(u):
@@ -122,13 +125,15 @@ def tile_rows_a_sigmoid_kb_mask_cap_kernel(tc, qT, kT, t, v, kb, mask, out):
         def quant_v():
             quantize(v_codes[:], v_scales[:], v_bf[:].rearrange("p h e j -> p (h e j)"))
 
-        mt = tile("mt", [P, PACK, NQ], F32)
+        mt = tile("mt", [P, 2, NQ, 2], F32)
 
-        def scale_mask(q0, w):
-            for r in range(PACK):
-                nc.vector.tensor_scalar(
-                    out=mt[:, r, q0 : q0 + w], in0=mask_raw[:, r, q0 : q0 + w], scalar1=t_sb[:, r : r + 1], scalar2=None, op0=ALU.mult
-                )
+        def scale_mask(u):
+            nc.vector.tensor_tensor(
+                out=mt[:, u],
+                in0=mask_raw[:, 2 * u : 2 * u + 2, :].rearrange("p l q -> p q l"),
+                in1=t_sb[:, u].to_broadcast([P, NQ, 2]),
+                op=ALU.mult,
+            )
 
         capped = [tile("capped%d" % n, [P, PACK, u[3]], F32) for n, u in enumerate(UNITS)]
         prob = {}
@@ -169,15 +174,15 @@ def tile_rows_a_sigmoid_kb_mask_cap_kernel(tc, qT, kT, t, v, kb, mask, out):
             )
 
         def sigmoid(n, c0, w):
-            prob[(n, c0)] = tile("prob%d_%d" % (n, c0), [P, PACK, w], F32)
-            nc.scalar.activation(out=prob[(n, c0)][:], in_=capped[n][:, :, c0 : c0 + w], func=ACT.Sigmoid, scale=2.0)
+            prob[(n, c0)] = tile("prob%d_%d" % (n, c0), [P, 2, w, 2], F32)
+            nc.scalar.activation(out=prob[(n, c0)][:], in_=capped[n][:, :, c0 : c0 + w].rearrange("p (u l) q -> p u q l", l=2), func=ACT.Sigmoid, scale=2.0)
 
         def weigh(n, c0, w):
             q0 = UNITS[n][2] + c0
             nc.vector.tensor_tensor(
-                out=w_bf[n][:, c0 : c0 + w, :].rearrange("p (c i) r -> p c r i", i=2),
-                in0=prob[(n, c0)][:].rearrange("p r (c i) -> p c r i", i=2),
-                in1=mt[:, :, q0 : q0 + w].rearrange("p r (c i) -> p c r i", i=2),
+                out=w_bf[n][:, c0 : c0 + w, :].rearrange("p q (u l) -> p q u l", l=2),
+                in0=prob[(n, c0)][:].rearrange("p u q l -> p q u l"),
+                in1=mt[:, :, q0 : q0 + w, :].rearrange("p u q l -> p q u l"),
                 op=ALU.mult,
             )
 
@@ -212,8 +217,8 @@ def tile_rows_a_sigmoid_kb_mask_cap_kernel(tc, qT, kT, t, v, kb, mask, out):
                 nc.vector.tensor_scalar(out=dst, in0=src, scalar1=1.0 / 16.0, scalar2=None, op0=ALU.mult)
             nc.sync.dma_start(out=out[h, q0 : q0 + w, :].rearrange("(c m) e -> m c e", m=MM), in_=y_sb[h][:, blocks, :])
 
-        halve_kb()
         cast_k(nc.vector.tensor_copy, 0)
+        halve_kb()
         cast_k(nc.scalar.copy, 1)
         cast_q(0, 0, 128)
         quant_k(0)
@@ -240,7 +245,8 @@ def tile_rows_a_sigmoid_kb_mask_cap_kernel(tc, qT, kT, t, v, kb, mask, out):
         cast_q(0,256,256)
         quant_q(0,128,128)
         quant_q(0,256,256)
-        scale_mask(0,512)
+        scale_mask(0)
+        scale_mask(1)
         sigmoid(0,0,128)
         sigmoid(1,0,128)
         scores2(2,0)
@@ -248,8 +254,6 @@ def tile_rows_a_sigmoid_kb_mask_cap_kernel(tc, qT, kT, t, v, kb, mask, out):
         scores2(2,2)
         weigh(0,0,128)
         weigh(1,0,128)
-        quant_w(0,0,128)
-        quant_w(1,0,128)
         cap(2,0)
         cap(3,0)
         scores2(2,3)
@@ -265,7 +269,6 @@ def tile_rows_a_sigmoid_kb_mask_cap_kernel(tc, qT, kT, t, v, kb, mask, out):
         cast_v(1)
         cast_q(1,256,256)
         quant_v()
-        quant_q(1,256,256)
         sigmoid(2,0,128)
         sigmoid(2,128,256)
         sigmoid(3,0,128)
@@ -273,13 +276,10 @@ def tile_rows_a_sigmoid_kb_mask_cap_kernel(tc, qT, kT, t, v, kb, mask, out):
         scores2(4,1)
         scores2(4,2)
         scores2(4,3)
-        scores(6,0)
-        scores(6,1)
-        scores(7,0)
-        scores(7,1)
-        scores(7,2)
-        scores(7,3)
         weigh(2,0,128)
+        quant_q(1,256,256)
+        quant_w(0,0,128)
+        quant_w(1,0,128)
         weigh(2,128,256)
         quant_w(2,0,128)
         weigh(3,0,128)
@@ -287,16 +287,18 @@ def tile_rows_a_sigmoid_kb_mask_cap_kernel(tc, qT, kT, t, v, kb, mask, out):
         cap(4,0)
         cap(4,1)
         sigmoid(3,128,256)
+        scores(6,0)
+        scores(6,1)
         scores(6,2)
         scores(6,3)
+        scores(7,0)
+        scores(7,1)
+        scores(7,2)
+        scores(7,3)
         values(0,0,128)
         values(2,0,384)
-        values(1,0,128)
         weigh(3,128,256)
         quant_w(3,0,128)
-        finish(1,0,512,0,0)
-        quant_w(3,128,256)
-        values(3,0,384)
         cap(4,2)
         cap(4,3)
         cap(5,0)
@@ -306,8 +308,11 @@ def tile_rows_a_sigmoid_kb_mask_cap_kernel(tc, qT, kT, t, v, kb, mask, out):
         scores(8,1)
         scores(8,2)
         scores(8,3)
+        quant_w(3,128,256)
+        values(1,0,128)
+        values(3,0,384)
         weigh(4,0,256)
-        finish(2,0,512,1,0)
+        finish(1,0,512,0,0)
         quant_w(4,0,256)
         values(4,0,256)
         cap(5,2)
@@ -315,17 +320,19 @@ def tile_rows_a_sigmoid_kb_mask_cap_kernel(tc, qT, kT, t, v, kb, mask, out):
         cap(6,0)
         sigmoid(5,0,256)
         weigh(5,0,256)
+        finish(2,0,512,1,0)
         quant_w(5,0,256)
         values(5,0,256)
         cap(6,1)
         cap(6,2)
         cap(6,3)
         cap(7,0)
-        cap(7,1)
         sigmoid(6,0,256)
         weigh(6,0,256)
+        finish(3,0,256,1,0)
         quant_w(6,0,256)
         values(6,0,256)
+        cap(7,1)
         cap(7,2)
         cap(7,3)
         cap(8,0)
@@ -342,7 +349,6 @@ def tile_rows_a_sigmoid_kb_mask_cap_kernel(tc, qT, kT, t, v, kb, mask, out):
         weigh(8,64,64)
         quant_w(7,0,128)
         quant_w(8,0,128)
-        finish(3,0,256,1,0,True)
         finish(0,0,512,0,0,True)
         values(7,0,128)
         values(8,0,128)

@@ -4,6 +4,8 @@ import concourse.mybir as mybir
 
 H, KV, D, NQ, N, E = 4, 2, 256, 512, 512, 128
 FLOPS = 2 * H * N * NQ * D + 2 * H * NQ * N * E
+CAP = 2.0
+OUT_SCALE = 1.0 / 16.0
 
 F32 = mybir.dt.float32
 BF16 = mybir.dt.bfloat16
@@ -18,11 +20,38 @@ ROWS = 64
 PACK = 4
 MM = 128
 BANK = 512
+SLOTS = range(PACK)
 
-UNITS = [[0,0,0,128],[0,1,0,128],[0,0,128,384],[0,1,128,384],[1,0,0,256],[1,1,0,256],[1,0,256,256],[1,1,256,128],[1,1,384,128]]
-PLACE = [[[0,0],[1,0],[2,0],[2,128]],[[0,0],[1,0],[2,0],[2,128]],[[0,0],[1,0],[2,0],[0,0]],[[0,0],[1,0],[2,0],[0,0]],[[1,0],[1,256],[2,0],[2,256]],[[1,0],[1,256],[2,0],[2,256]],[[0,0],[0,256],[1,0],[1,256]],[[0,0],[0,128],[0,256],[0,384]],[[1,0],[1,128],[1,256],[1,384]]]
-Y_PLACE = [(0, 0), (1, 0), (0, 128), (1, 128), (0, 0), (1, 0), (0, 256), (1, 256), (0, 0)]
-HEAD = [[1, 2], [0, 3]]
+PAIR_HEADS = [[1, 2], [0, 3]]
+
+Q_LOADS = [(0, 0, 128), (0, 128, 384), (1, 0, 256), (1, 256, 256)]
+MASK_COLS = 256
+
+UNITS = [
+    (0, 0, 0, 128),
+    (0, 1, 0, 128),
+    (0, 0, 128, 384),
+    (0, 1, 128, 384),
+    (1, 0, 0, 256),
+    (1, 1, 0, 256),
+    (1, 0, 256, 256),
+    (1, 1, 256, 128),
+    (1, 1, 384, 128),
+]
+
+SCORE_PLACE = [
+    [(0, 0), (1, 0), (2, 0), (2, 128)],
+    [(0, 0), (1, 0), (2, 0), (2, 128)],
+    [(0, 0), (1, 0), (2, 0), (0, 0)],
+    [(0, 0), (1, 0), (2, 0), (0, 0)],
+    [(1, 0), (1, 256), (2, 0), (2, 256)],
+    [(1, 0), (1, 256), (2, 0), (2, 256)],
+    [(0, 0), (0, 256), (1, 0), (1, 256)],
+    [(0, 0), (0, 128), (0, 256), (0, 384)],
+    [(1, 0), (1, 128), (1, 256), (1, 384)],
+]
+
+Y_PLACE = [(g, q0) for pair, g, q0, width in UNITS[:-1]] + [(0, 0)]
 
 
 def tile_rows_a_sigmoid_kb_mask_cap_kernel(tc, qT, kT, t, v, kb, mask, out):
@@ -35,57 +64,64 @@ def tile_rows_a_sigmoid_kb_mask_cap_kernel(tc, qT, kT, t, v, kb, mask, out):
         def tile(name, shape, dtype):
             return sb.tile(shape, dtype, name=name, align_bytes=64)
 
-        score_banks = [[ps.tile([P, BANK], F32, name="score%d_%d" % (g, b)) for b in range(3)] for g in range(2)]
+        score_banks = [[ps.tile([P, BANK], F32, name="score%d_%d" % (g, b)) for b in range(3)] for g in range(KV)]
         y_banks = [ps.tile([P, BANK], F32, name="y%d" % b) for b in range(2)]
 
         k_raw = tile("k_raw", [P, PACK, N], F32)
         kb_sb = tile("kb_sb", [P, PACK], F32)
-        t_sb = tile("t_sb", [P, 2, 1, 2], F32)
+        t_sb = tile("t_sb", [P, PACK], F32)
         v_raw = tile("v_raw", [P, KV, PACK, E], F32)
-        q_rows = qT.rearrange("h d n -> (h d) n")
-        q_raw = {(0, 0): tile("q_raw_a", [P, PACK, 128], F32), (0, 128): tile("q_raw_b", [P, PACK, 384], F32), (1, 0): tile("q_raw_c", [P, PACK, NQ], F32)}
-        mask_raw = tile("mask_raw", [P, PACK, NQ], F32)
+        q_raw = {(pair, q0): tile("q_raw%d_%d" % (pair, q0), [P, PACK, width], F32) for pair, q0, width in Q_LOADS}
+        mask_raw = {q0: tile("mask_raw%d" % q0, [P, PACK, MASK_COLS], F32) for q0 in range(0, NQ, MASK_COLS)}
 
-        def load_q0(q0, w):
-            nc.sync.dma_start(
-                out=q_raw[(0, q0)][:], in_=q_rows[D : 3 * D, q0 : q0 + w].rearrange("(p j) n -> p j n", j=PACK)
-            )
+        def load_mask(q0):
+            nc.sync.dma_start(out=mask_raw[q0][:], in_=mask[:, q0 : q0 + MASK_COLS].rearrange("(p j) n -> p j n", j=PACK))
 
-        def load_q1(queue, g):
-            queue.dma_start(
-                out=q_raw[(1, 0)][ROWS * g : ROWS * (g + 1)], in_=qT[HEAD[1][g]].rearrange("(p j) n -> p j n", j=PACK)
-            )
+        def load_second_pair_head(queue, g):
+            for pair, q0, width in Q_LOADS[2:]:
+                queue.dma_start(
+                    out=q_raw[(pair, q0)][ROWS * g : ROWS * (g + 1)],
+                    in_=qT[PAIR_HEADS[pair][g], :, q0 : q0 + width].rearrange("(p j) n -> p j n", j=PACK),
+                )
 
         nc.scalar.dma_start(out=kb_sb[:], in_=kb.rearrange("(p j) o -> p (j o)", j=PACK))
-        nc.scalar.dma_start(out=t_sb[:].rearrange("p u o l -> p (u o l)"), in_=t.rearrange("(p j) o -> p (j o)", j=PACK))
+        nc.scalar.dma_start(out=t_sb[:], in_=t.rearrange("(p j) o -> p (j o)", j=PACK))
         nc.sync.dma_start(out=k_raw[:], in_=kT.rearrange("h (p j) n -> (h p) j n", j=PACK))
-        load_q0(0, 128)
-        load_q0(128, 384)
-        for u in range(2):
+        first_pair_rows = qT.rearrange("h d n -> (h d) n")[D : 3 * D]
+        for pair, q0, width in Q_LOADS[:2]:
             nc.sync.dma_start(
-                out=mask_raw[:, 2 * u : 2 * u + 2, :], in_=mask.rearrange("(p j) n -> p j n", j=PACK)[:, 2 * u : 2 * u + 2, :]
+                out=q_raw[(pair, q0)][:], in_=first_pair_rows[:, q0 : q0 + width].rearrange("(p j) n -> p j n", j=PACK)
             )
-        load_q1(nc.sync, 0)
+        load_mask(0)
         nc.sync.dma_start(out=v_raw[:], in_=v.rearrange("h (p j) e -> p h j e", j=PACK))
+        load_mask(MASK_COLS)
+        load_second_pair_head(nc.sync, 0)
 
-        warm = tile("warm", [P, 8], F32)
+        warm_in = tile("warm_in", [P, 8], F32)
         warm_out = tile("warm_out", [P, 8], F32)
-        nc.vector.memset(warm[:], 0.0)
-        nc.scalar.activation(out=warm_out[:], in_=warm[:], func=ACT.Sigmoid)
+        nc.vector.memset(warm_in[:], 0.0)
+        nc.scalar.activation(out=warm_out[:], in_=warm_in[:], func=ACT.Sigmoid)
 
-        kb_half = tile("kb_half", [P, PACK], F32)
+        def quantize(codes, scales, values):
+            nc.vector.quantize_mx(out=codes.bitcast(FP8X4), scales=scales, in_=values)
 
-        def halve_kb():
-            nc.vector.tensor_scalar(out=kb_half[:], in0=kb_sb[:], scalar1=0.5, scalar2=None, op0=ALU.mult)
+        def cast_interleaved(dst, src):
+            nc.vector.tensor_copy(
+                out=dst.rearrange("p (c i) j -> p c j i", i=2), in_=src.rearrange("p j (c i) -> p c j i", i=2)
+            )
 
-        def load_h3():
-            load_q1(nc.scalar, 1)
+        def product(dst, lhs_codes, lhs_scales, rhs_codes, rhs_scales):
+            nc.tensor.matmul_mx(
+                out=dst,
+                lhsT=lhs_codes.bitcast(FP8X4),
+                lhsT_scale=lhs_scales,
+                rhs=rhs_codes.bitcast(FP8X4),
+                rhs_scale=rhs_scales,
+                start=True,
+                stop=True,
+            )
 
-        def interleave(eng_copy, dst, src):
-            eng_copy(out=dst.rearrange("p (c i) j -> p c j i", i=2), in_=src.rearrange("p j (c i) -> p c j i", i=2))
-
-        def quantize(codes, scales, src):
-            nc.vector.quantize_mx(out=codes.bitcast(FP8X4), scales=scales, in_=src)
+        kb_bias = tile("kb_bias", [P, PACK], F32)
 
         k_bf = [tile("k_bf%d" % u, [P, 2, MM, PACK], BF16) for u in range(2)]
         k_codes = [tile("k_codes%d" % u, [P, 2 * MM], U32) for u in range(2)]
@@ -93,264 +129,208 @@ def tile_rows_a_sigmoid_kb_mask_cap_kernel(tc, qT, kT, t, v, kb, mask, out):
 
         def cast_k(copy, u):
             copy(
-                out=k_bf[u][:].rearrange("p i s j -> p s i j"),
-                in_=k_raw[:].rearrange("p j (s u i) -> p u s i j", u=2, i=2)[:, u],
+                out=k_bf[u][:].rearrange("p i s j -> p s j i"),
+                in_=k_raw[:].rearrange("p j (s u i) -> p u s j i", u=2, i=2)[:, u],
             )
 
         def quant_k(u):
             quantize(k_codes[u][:], k_scales[u][:], k_bf[u][:].rearrange("p i s j -> p (i s j)"))
 
-        q_bf = [tile("q_bf%d" % a, [P, NQ, PACK], BF16) for a in range(2)]
-        q_codes = [tile("q_codes%d" % a, [P, NQ], U32) for a in range(2)]
-        q_scales = [tile("q_scales%d" % a, [P, NQ], U8) for a in range(2)]
+        q_bf = [tile("q_bf%d" % pair, [P, NQ, PACK], BF16) for pair in range(2)]
+        q_codes = [tile("q_codes%d" % pair, [P, NQ], U32) for pair in range(2)]
+        q_scales = [tile("q_scales%d" % pair, [P, NQ], U8) for pair in range(2)]
 
-        def cast_q(pair, q0, w):
-            first = 128 if pair == 0 and q0 >= 128 else 0
-            interleave(nc.vector.tensor_copy, q_bf[pair][:, q0 : q0 + w, :], q_raw[(pair, first)][:, :, q0 - first : q0 - first + w])
+        def cast_q(pair, q0, width):
+            load0 = max(first for load_pair, first in q_raw if load_pair == pair and first <= q0)
+            cast_interleaved(q_bf[pair][:, q0 : q0 + width, :], q_raw[(pair, load0)][:, :, q0 - load0 : q0 - load0 + width])
 
-        def quant_q(pair, q0, w):
-            quantize(
-                q_codes[pair][:, q0 : q0 + w],
-                q_scales[pair][:, q0 : q0 + w],
-                q_bf[pair][:, q0 : q0 + w, :].rearrange("p n j -> p (n j)"),
-            )
+        def quant_q(pair, q0, width):
+            cols = slice(q0, q0 + width)
+            quantize(q_codes[pair][:, cols], q_scales[pair][:, cols], q_bf[pair][:, cols, :].rearrange("p n j -> p (n j)"))
 
         v_bf = tile("v_bf", [P, KV, E, PACK], BF16)
         v_codes = tile("v_codes", [P, KV * E], U32)
         v_scales = tile("v_scales", [P, KV * E], U8)
 
-        def cast_v(g):
-            interleave(nc.vector.tensor_copy, v_bf[:, g], v_raw[:, g])
+        mask_t = tile("mask_t", [P, PACK, NQ], F32)
 
-        def quant_v():
-            quantize(v_codes[:], v_scales[:], v_bf[:].rearrange("p h e j -> p (h e j)"))
+        def scale_mask(q0):
+            for r in SLOTS:
+                nc.vector.tensor_scalar(
+                    out=mask_t[:, r, q0 : q0 + MASK_COLS],
+                    in0=mask_raw[q0][:, r, :],
+                    scalar1=t_sb[:, r : r + 1],
+                    scalar2=None,
+                    op0=ALU.mult,
+                )
 
-        mt = tile("mt", [P, 2, NQ, 2], F32)
-
-        def scale_mask(u):
-            nc.vector.tensor_tensor(
-                out=mt[:, u],
-                in0=mask_raw[:, 2 * u : 2 * u + 2, :].rearrange("p l q -> p q l"),
-                in1=t_sb[:, u].to_broadcast([P, NQ, 2]),
-                op=ALU.mult,
-            )
-
-        capped = [tile("capped%d" % n, [P, PACK, u[3]], F32) for n, u in enumerate(UNITS)]
+        capped = [tile("capped%d" % n, [P, PACK, unit[3]], F32) for n, unit in enumerate(UNITS)]
         prob = {}
-        w_bf = [tile("w_bf%d" % n, [P, u[3], PACK], BF16) for n, u in enumerate(UNITS)]
-        w_codes = [tile("w_codes%d" % n, [P, u[3]], U32) for n, u in enumerate(UNITS)]
-        w_scales = [tile("w_scales%d" % n, [P, u[3]], U8) for n, u in enumerate(UNITS)]
+        w_bf = [tile("w_bf%d" % n, [P, unit[3], PACK], BF16) for n, unit in enumerate(UNITS)]
+        w_codes = [tile("w_codes%d" % n, [P, unit[3]], U32) for n, unit in enumerate(UNITS)]
+        w_scales = [tile("w_scales%d" % n, [P, unit[3]], U8) for n, unit in enumerate(UNITS)]
         y_sb = [tile("y_sb%d" % h, [P, NQ // MM, E], F32) for h in range(H)]
 
-        place = {(n, r): (score_banks[UNITS[n][1]][b], c) for n in range(len(UNITS)) for r, (b, c) in enumerate(PLACE[n])}
-
-        def scores2(n, r):
-            for c in range(0, UNITS[n][3], MM):
-                scores(n, r, c)
-                scores(n + 1, r, c)
-
-        def scores(n, r, only=None):
-            pair, g, q0, w = UNITS[n]
-            bank, c0 = place[(n, r)]
+        def scores(n, r):
+            pair, g, q0, width = UNITS[n]
+            bank, col0 = SCORE_PLACE[n][r]
             rows = slice(ROWS * g, ROWS * (g + 1))
-            kc = slice((r % 2) * MM, (r % 2 + 1) * MM)
-            for c in (range(0, w, MM) if only is None else [only]):
-                qc = slice(q0 + c, q0 + c + MM)
-                nc.tensor.matmul_mx(
-                    out=bank[:, c0 + c : c0 + c + MM],
-                    lhsT=k_codes[r // 2][rows, kc].bitcast(FP8X4),
-                    lhsT_scale=k_scales[r // 2][rows, kc],
-                    rhs=q_codes[pair][rows, qc].bitcast(FP8X4),
-                    rhs_scale=q_scales[pair][rows, qc],
-                    start=True,
-                    stop=True,
+            k_cols = slice((r % 2) * MM, (r % 2 + 1) * MM)
+            for c in range(0, width, MM):
+                q_cols = slice(q0 + c, q0 + c + MM)
+                product(
+                    score_banks[g][bank][:, col0 + c : col0 + c + MM],
+                    k_codes[r // 2][rows, k_cols],
+                    k_scales[r // 2][rows, k_cols],
+                    q_codes[pair][rows, q_cols],
+                    q_scales[pair][rows, q_cols],
                 )
 
         def cap(n, r):
-            w = UNITS[n][3]
-            bank, c0 = place[(n, r)]
+            pair, g, q0, width = UNITS[n]
+            bank, col0 = SCORE_PLACE[n][r]
             nc.scalar.activation(
-                out=capped[n][:, r, :], in_=bank[:, c0 : c0 + w], func=ACT.Tanh, bias=kb_half[:, r : r + 1], scale=0.5
+                out=capped[n][:, r, :],
+                in_=score_banks[g][bank][:, col0 : col0 + width],
+                func=ACT.Tanh,
+                bias=kb_bias[:, r : r + 1],
+                scale=1.0 / CAP,
             )
 
-        def sigmoid(n, c0, w):
-            prob[(n, c0)] = tile("prob%d_%d" % (n, c0), [P, 2, w, 2], F32)
-            nc.scalar.activation(out=prob[(n, c0)][:], in_=capped[n][:, :, c0 : c0 + w].rearrange("p (u l) q -> p u q l", l=2), func=ACT.Sigmoid, scale=2.0)
+        def sigmoid(n, c0, width):
+            prob[(n, c0)] = tile("prob%d_%d" % (n, c0), [P, PACK, width], F32)
+            nc.scalar.activation(out=prob[(n, c0)][:], in_=capped[n][:, :, c0 : c0 + width], func=ACT.Sigmoid, scale=CAP)
 
-        def weigh(n, c0, w):
+        def weigh(n, c0, width):
             q0 = UNITS[n][2] + c0
             nc.vector.tensor_tensor(
-                out=w_bf[n][:, c0 : c0 + w, :].rearrange("p q (u l) -> p q u l", l=2),
-                in0=prob[(n, c0)][:].rearrange("p u q l -> p q u l"),
-                in1=mt[:, :, q0 : q0 + w, :].rearrange("p u q l -> p q u l"),
+                out=w_bf[n][:, c0 : c0 + width, :].rearrange("p (c i) r -> p c r i", i=2),
+                in0=prob[(n, c0)][:].rearrange("p r (c i) -> p c r i", i=2),
+                in1=mask_t[:, :, q0 : q0 + width].rearrange("p r (c i) -> p c r i", i=2),
                 op=ALU.mult,
             )
 
-        def quant_w(n, c0, w):
-            quantize(
-                w_codes[n][:, c0 : c0 + w],
-                w_scales[n][:, c0 : c0 + w],
-                w_bf[n][:, c0 : c0 + w, :].rearrange("p n r -> p (n r)"),
-            )
+        def quant_w(n, c0, width):
+            cols = slice(c0, c0 + width)
+            quantize(w_codes[n][:, cols], w_scales[n][:, cols], w_bf[n][:, cols, :].rearrange("p q r -> p (q r)"))
 
-        def values(n, c0, w):
-            g = UNITS[n][1]
-            vc = slice(g * E, (g + 1) * E)
-            for c in range(c0, c0 + w, MM):
-                nc.tensor.matmul_mx(
-                    out=y_banks[Y_PLACE[n][0]][:, Y_PLACE[n][1] + c : Y_PLACE[n][1] + c + E],
-                    lhsT=w_codes[n][:, c : c + MM].bitcast(FP8X4),
-                    lhsT_scale=w_scales[n][:, c : c + MM],
-                    rhs=v_codes[:, vc].bitcast(FP8X4),
-                    rhs_scale=v_scales[:, vc],
-                    start=True,
-                    stop=True,
+        def values(n):
+            pair, g, q0, width = UNITS[n]
+            bank, col0 = Y_PLACE[n]
+            v_cols = slice(g * E, (g + 1) * E)
+            for c in range(0, width, MM):
+                product(
+                    y_banks[bank][:, col0 + c : col0 + c + E],
+                    w_codes[n][:, c : c + MM],
+                    w_scales[n][:, c : c + MM],
+                    v_codes[:, v_cols],
+                    v_scales[:, v_cols],
                 )
 
-        def finish(h, q0, w, bank, c0, on_scalar=False):
-            blocks = slice(q0 // MM, (q0 + w) // MM)
-            dst = y_sb[h][:, blocks, :].rearrange("p c e -> p (c e)")
-            src = y_banks[bank][:, c0 : c0 + w]
+        def finish(first, last, on_scalar):
+            pair, g, q0 = UNITS[first][:3]
+            width = UNITS[last][2] + UNITS[last][3] - q0
+            bank, col0 = Y_PLACE[first]
+            head = PAIR_HEADS[pair][g]
+            staged = y_sb[head][:, q0 // MM : (q0 + width) // MM, :]
+            dst = staged.rearrange("p c e -> p (c e)")
+            src = y_banks[bank][:, col0 : col0 + width]
             if on_scalar:
-                nc.scalar.activation(out=dst, in_=src, func=ACT.Copy, scale=1.0 / 16.0)
+                nc.scalar.activation(out=dst, in_=src, func=ACT.Copy, scale=OUT_SCALE)
             else:
-                nc.vector.tensor_scalar(out=dst, in0=src, scalar1=1.0 / 16.0, scalar2=None, op0=ALU.mult)
-            nc.sync.dma_start(out=out[h, q0 : q0 + w, :].rearrange("(c m) e -> m c e", m=MM), in_=y_sb[h][:, blocks, :])
+                nc.vector.tensor_scalar(out=dst, in0=src, scalar1=OUT_SCALE, scalar2=None, op0=ALU.mult)
+            nc.sync.dma_start(out=out[head, q0 : q0 + width, :].rearrange("(c m) e -> m c e", m=MM), in_=staged)
+
+        def each(step, places):
+            for place in places:
+                step(*place)
+
+        def all_slots(*units):
+            return [(n, r) for n in units for r in SLOTS]
+
 
         cast_k(nc.vector.tensor_copy, 0)
-        halve_kb()
+        nc.vector.tensor_scalar(out=kb_bias[:], in0=kb_sb[:], scalar1=1.0 / CAP, scalar2=None, op0=ALU.mult)
         cast_k(nc.scalar.copy, 1)
         cast_q(0, 0, 128)
         quant_k(0)
         quant_q(0, 0, 128)
         quant_k(1)
-        scores(0,0)
-        scores(1,0)
-        scores(0,1)
-        scores(1,1)
-        scores(0,2)
-        scores(0,3)
-        scores(1,2)
-        scores(1,3)
-        cap(0,0)
-        cap(1,0)
-        cap(0,1)
-        cap(1,1)
-        load_h3()
-        cap(0,2)
-        cap(0,3)
-        cap(1,2)
-        cap(1,3)
-        cast_q(0,128,128)
-        cast_q(0,256,256)
-        quant_q(0,128,128)
-        quant_q(0,256,256)
+        opening = [(0, 0), (1, 0), (0, 1), (1, 1), (0, 2), (0, 3), (1, 2), (1, 3)]
+        each(scores, opening)
+        each(cap, opening)
+        wide_pieces = [(0, 128), (128, 256)]
+        each(cast_q, [(0, 128 + c0, width) for c0, width in wide_pieces])
+        each(quant_q, [(0, 128 + c0, width) for c0, width in wide_pieces])
         scale_mask(0)
-        scale_mask(1)
-        sigmoid(0,0,128)
-        sigmoid(1,0,128)
-        scores2(2,0)
-        scores2(2,1)
-        scores2(2,2)
-        weigh(0,0,128)
-        weigh(1,0,128)
-        cap(2,0)
-        cap(3,0)
-        scores2(2,3)
-        cap(2,1)
-        cap(3,1)
-        cap(2,2)
-        cap(3,2)
-        cap(2,3)
-        cap(3,3)
-        cast_q(1,0,256)
-        cast_v(0)
-        quant_q(1,0,256)
-        cast_v(1)
-        cast_q(1,256,256)
-        quant_v()
-        sigmoid(2,0,128)
-        sigmoid(2,128,256)
-        sigmoid(3,0,128)
-        scores2(4,0)
-        scores2(4,1)
-        scores2(4,2)
-        scores2(4,3)
-        weigh(2,0,128)
-        quant_q(1,256,256)
-        quant_w(0,0,128)
-        quant_w(1,0,128)
-        weigh(2,128,256)
-        quant_w(2,0,128)
-        weigh(3,0,128)
-        quant_w(2,128,256)
-        cap(4,0)
-        cap(4,1)
-        sigmoid(3,128,256)
-        scores(6,0)
-        scores(6,1)
-        scores(6,2)
-        scores(6,3)
-        scores(7,0)
-        scores(7,1)
-        scores(7,2)
-        scores(7,3)
-        values(0,0,128)
-        values(2,0,384)
-        weigh(3,128,256)
-        quant_w(3,0,128)
-        cap(4,2)
-        cap(4,3)
-        cap(5,0)
-        cap(5,1)
-        sigmoid(4,0,256)
-        scores(8,0)
-        scores(8,1)
-        scores(8,2)
-        scores(8,3)
-        quant_w(3,128,256)
-        values(1,0,128)
-        values(3,0,384)
-        weigh(4,0,256)
-        finish(1,0,512,0,0)
-        quant_w(4,0,256)
-        values(4,0,256)
-        cap(5,2)
-        cap(5,3)
-        cap(6,0)
-        sigmoid(5,0,256)
-        weigh(5,0,256)
-        finish(2,0,512,1,0)
-        quant_w(5,0,256)
-        values(5,0,256)
-        cap(6,1)
-        cap(6,2)
-        cap(6,3)
-        cap(7,0)
-        sigmoid(6,0,256)
-        weigh(6,0,256)
-        finish(3,0,256,1,0)
-        quant_w(6,0,256)
-        values(6,0,256)
-        cap(7,1)
-        cap(7,2)
-        cap(7,3)
-        cap(8,0)
-        cap(8,1)
-        sigmoid(7,0,64)
-        cap(8,2)
-        cap(8,3)
-        sigmoid(7,64,64)
-        sigmoid(8,0,64)
-        sigmoid(8,64,64)
-        weigh(7,0,64)
-        weigh(7,64,64)
-        weigh(8,0,64)
-        weigh(8,64,64)
-        quant_w(7,0,128)
-        quant_w(8,0,128)
-        finish(0,0,512,0,0,True)
-        values(7,0,128)
-        values(8,0,128)
-        finish(3,256,128,1,256)
-        finish(3,384,128,0,0,True)
+        sigmoid(0, 0, 128)
+        load_second_pair_head(nc.scalar, 1)
+        sigmoid(1, 0, 128)
+
+        each(scores, [(2, 0), (2, 1), (3, 0), (2, 2)])
+        weigh(0, 0, 128)
+        for g in range(KV):
+            cast_interleaved(v_bf[:, g], v_raw[:, g])
+        weigh(1, 0, 128)
+        quant_w(0, 0, 128)
+        scale_mask(MASK_COLS)
+        quant_w(1, 0, 128)
+        quantize(v_codes[:], v_scales[:], v_bf[:].rearrange("p g e r -> p (g e r)"))
+        cap(2, 0)
+        each(scores, [(2, 3), (3, 1), (3, 2)])
+        each(cap, [(2, 1), (3, 0)])
+        scores(3, 3)
+        each(cap, [(2, 2), (2, 3), (3, 1)])
+        sigmoid(2, 0, 128)
+        each(cap, [(3, 2), (3, 3)])
+        each(sigmoid, [(2, 128, 256), (3, 0, 128), (3, 128, 256)])
+        weigh(2, 0, 128)
+        cast_q(1, 0, 256)
+        quant_w(2, 0, 128)
+        quant_q(1, 0, 256)
+        weigh(2, 128, 256)
+        weigh(3, 0, 128)
+        cast_q(1, 256, 256)
+        quant_w(3, 0, 128)
+        quant_w(2, 128, 256)
+        quant_q(1, 256, 256)
+
+        each(scores, all_slots(4, 5))
+        values(0)
+        values(2)
+        weigh(3, 128, 256)
+        finish(0, 2, on_scalar=False)
+        quant_w(3, 128, 256)
+        each(cap, all_slots(4, 5)[:6])
+        each(scores, all_slots(6, 7, 8))
+        values(1)
+        values(3)
+        each(cap, all_slots(4, 5)[6:])
+        each(sigmoid, [(4, 0, 256), (5, 0, 256)])
+        each(weigh, [(4, 0, 256), (5, 0, 256)])
+        quant_w(4, 0, 256)
+        finish(1, 3, on_scalar=False)
+        quant_w(5, 0, 256)
+        values(4)
+        values(5)
+
+        each(cap, all_slots(6) + [(7, 0)])
+        sigmoid(6, 0, 256)
+        weigh(6, 0, 256)
+        quant_w(6, 0, 256)
+        values(6)
+        halves = [(n, c0, 64) for n in (7, 8) for c0 in (0, 64)]
+        each(cap, all_slots(7, 8)[1:6])
+        sigmoid(*halves[0])
+        each(cap, all_slots(7, 8)[6:])
+        each(sigmoid, halves[1:])
+        each(weigh, halves)
+        quant_w(7, 0, 128)
+        quant_w(8, 0, 128)
+
+        finish(5, 5, on_scalar=True)
+        finish(4, 6, on_scalar=True)
+        values(7)
+        values(8)
+        finish(7, 7, on_scalar=False)
+        finish(8, 8, on_scalar=True)

from contextlib import ExitStack

import concourse.mybir as mybir

H, KV, D, NQ, N, E = 4, 2, 256, 512, 512, 128
FLOPS = 2 * H * N * NQ * D + 2 * H * NQ * N * E
CAP = 2.0
OUT_SCALE = 1.0 / 16.0

F32 = mybir.dt.float32
BF16 = mybir.dt.bfloat16
U32 = mybir.dt.uint32
U8 = mybir.dt.uint8
FP8X4 = mybir.dt.float8_e4m3fn_x4
ACT = mybir.ActivationFunctionType
ALU = mybir.AluOpType

P = 128
ROWS = 64
PACK = 4
MM = 128
BANK = 512
SLOTS = range(PACK)

PAIR_HEADS = [[1, 2], [0, 3]]

Q_LOADS = [(0, 0, 128), (0, 128, 384), (1, 0, 256), (1, 256, 256)]
MASK_COLS = 256

UNITS = [
    (0, 0, 0, 128),
    (0, 1, 0, 128),
    (0, 0, 128, 384),
    (0, 1, 128, 384),
    (1, 0, 0, 256),
    (1, 1, 0, 256),
    (1, 0, 256, 256),
    (1, 1, 256, 128),
    (1, 1, 384, 128),
]

SCORE_PLACE = [
    [(0, 0), (1, 0), (2, 0), (2, 128)],
    [(0, 0), (1, 0), (2, 0), (2, 128)],
    [(0, 0), (1, 0), (2, 0), (0, 0)],
    [(0, 0), (1, 0), (2, 0), (0, 0)],
    [(1, 0), (1, 256), (2, 0), (2, 256)],
    [(1, 0), (1, 256), (2, 0), (2, 256)],
    [(0, 0), (0, 256), (1, 0), (1, 256)],
    [(0, 0), (0, 128), (0, 256), (0, 384)],
    [(1, 0), (1, 128), (1, 256), (1, 384)],
]

Y_PLACE = [(g, q0) for pair, g, q0, width in UNITS[:-1]] + [(0, 0)]


def tile_rows_a_sigmoid_kb_mask_cap_kernel(tc, qT, kT, t, v, kb, mask, out):
    nc = tc.nc
    with ExitStack() as ctx:
        sb = ctx.enter_context(tc.tile_pool(name="sb", bufs=1))
        ps = ctx.enter_context(tc.psum_pool(name="ps", bufs=1))
        ctx.enter_context(tc.manual_schedule())

        def tile(name, shape, dtype):
            return sb.tile(shape, dtype, name=name, align_bytes=64)

        score_banks = [[ps.tile([P, BANK], F32, name="score%d_%d" % (g, b)) for b in range(3)] for g in range(KV)]
        y_banks = [ps.tile([P, BANK], F32, name="y%d" % b) for b in range(2)]

        k_raw = tile("k_raw", [P, PACK, N], F32)
        kb_sb = tile("kb_sb", [P, PACK], F32)
        t_sb = tile("t_sb", [P, PACK], F32)
        v_raw = tile("v_raw", [P, KV, PACK, E], F32)
        q_raw = {(pair, q0): tile("q_raw%d_%d" % (pair, q0), [P, PACK, width], F32) for pair, q0, width in Q_LOADS}
        mask_raw = {q0: tile("mask_raw%d" % q0, [P, PACK, MASK_COLS], F32) for q0 in range(0, NQ, MASK_COLS)}

        def load_mask(q0):
            nc.sync.dma_start(out=mask_raw[q0][:], in_=mask[:, q0 : q0 + MASK_COLS].rearrange("(p j) n -> p j n", j=PACK))

        def load_second_pair_head(queue, g):
            for pair, q0, width in Q_LOADS[2:]:
                queue.dma_start(
                    out=q_raw[(pair, q0)][ROWS * g : ROWS * (g + 1)],
                    in_=qT[PAIR_HEADS[pair][g], :, q0 : q0 + width].rearrange("(p j) n -> p j n", j=PACK),
                )

        nc.scalar.dma_start(out=kb_sb[:], in_=kb.rearrange("(p j) o -> p (j o)", j=PACK))
        nc.scalar.dma_start(out=t_sb[:], in_=t.rearrange("(p j) o -> p (j o)", j=PACK))
        nc.sync.dma_start(out=k_raw[:], in_=kT.rearrange("h (p j) n -> (h p) j n", j=PACK))
        first_pair_rows = qT.rearrange("h d n -> (h d) n")[D : 3 * D]
        for pair, q0, width in Q_LOADS[:2]:
            nc.sync.dma_start(
                out=q_raw[(pair, q0)][:], in_=first_pair_rows[:, q0 : q0 + width].rearrange("(p j) n -> p j n", j=PACK)
            )
        load_mask(0)
        nc.sync.dma_start(out=v_raw[:], in_=v.rearrange("h (p j) e -> p h j e", j=PACK))
        load_mask(MASK_COLS)
        load_second_pair_head(nc.sync, 0)

        warm_in = tile("warm_in", [P, 8], F32)
        warm_out = tile("warm_out", [P, 8], F32)
        nc.vector.memset(warm_in[:], 0.0)
        nc.scalar.activation(out=warm_out[:], in_=warm_in[:], func=ACT.Sigmoid)

        def quantize(codes, scales, values):
            nc.vector.quantize_mx(out=codes.bitcast(FP8X4), scales=scales, in_=values)

        def cast_interleaved(dst, src):
            nc.vector.tensor_copy(
                out=dst.rearrange("p (c i) j -> p c j i", i=2), in_=src.rearrange("p j (c i) -> p c j i", i=2)
            )

        def product(dst, lhs_codes, lhs_scales, rhs_codes, rhs_scales):
            nc.tensor.matmul_mx(
                out=dst,
                lhsT=lhs_codes.bitcast(FP8X4),
                lhsT_scale=lhs_scales,
                rhs=rhs_codes.bitcast(FP8X4),
                rhs_scale=rhs_scales,
                start=True,
                stop=True,
            )

        kb_bias = tile("kb_bias", [P, PACK], F32)

        k_bf = [tile("k_bf%d" % u, [P, 2, MM, PACK], BF16) for u in range(2)]
        k_codes = [tile("k_codes%d" % u, [P, 2 * MM], U32) for u in range(2)]
        k_scales = [tile("k_scales%d" % u, [P, 2 * MM], U8) for u in range(2)]

        def cast_k(copy, u):
            copy(
                out=k_bf[u][:].rearrange("p i s j -> p s j i"),
                in_=k_raw[:].rearrange("p j (s u i) -> p u s j i", u=2, i=2)[:, u],
            )

        def quant_k(u):
            quantize(k_codes[u][:], k_scales[u][:], k_bf[u][:].rearrange("p i s j -> p (i s j)"))

        q_bf = [tile("q_bf%d" % pair, [P, NQ, PACK], BF16) for pair in range(2)]
        q_codes = [tile("q_codes%d" % pair, [P, NQ], U32) for pair in range(2)]
        q_scales = [tile("q_scales%d" % pair, [P, NQ], U8) for pair in range(2)]

        def cast_q(pair, q0, width):
            load0 = max(first for load_pair, first in q_raw if load_pair == pair and first <= q0)
            cast_interleaved(q_bf[pair][:, q0 : q0 + width, :], q_raw[(pair, load0)][:, :, q0 - load0 : q0 - load0 + width])

        def quant_q(pair, q0, width):
            cols = slice(q0, q0 + width)
            quantize(q_codes[pair][:, cols], q_scales[pair][:, cols], q_bf[pair][:, cols, :].rearrange("p n j -> p (n j)"))

        v_bf = tile("v_bf", [P, KV, E, PACK], BF16)
        v_codes = tile("v_codes", [P, KV * E], U32)
        v_scales = tile("v_scales", [P, KV * E], U8)

        mask_t = tile("mask_t", [P, PACK, NQ], F32)

        def scale_mask(q0):
            for r in SLOTS:
                nc.vector.tensor_scalar(
                    out=mask_t[:, r, q0 : q0 + MASK_COLS],
                    in0=mask_raw[q0][:, r, :],
                    scalar1=t_sb[:, r : r + 1],
                    scalar2=None,
                    op0=ALU.mult,
                )

        capped = [tile("capped%d" % n, [P, PACK, unit[3]], F32) for n, unit in enumerate(UNITS)]
        prob = {}
        w_bf = [tile("w_bf%d" % n, [P, unit[3], PACK], BF16) for n, unit in enumerate(UNITS)]
        w_codes = [tile("w_codes%d" % n, [P, unit[3]], U32) for n, unit in enumerate(UNITS)]
        w_scales = [tile("w_scales%d" % n, [P, unit[3]], U8) for n, unit in enumerate(UNITS)]
        y_sb = [tile("y_sb%d" % h, [P, NQ // MM, E], F32) for h in range(H)]

        def scores(n, r):
            pair, g, q0, width = UNITS[n]
            bank, col0 = SCORE_PLACE[n][r]
            rows = slice(ROWS * g, ROWS * (g + 1))
            k_cols = slice((r % 2) * MM, (r % 2 + 1) * MM)
            for c in range(0, width, MM):
                q_cols = slice(q0 + c, q0 + c + MM)
                product(
                    score_banks[g][bank][:, col0 + c : col0 + c + MM],
                    k_codes[r // 2][rows, k_cols],
                    k_scales[r // 2][rows, k_cols],
                    q_codes[pair][rows, q_cols],
                    q_scales[pair][rows, q_cols],
                )

        def cap(n, r):
            pair, g, q0, width = UNITS[n]
            bank, col0 = SCORE_PLACE[n][r]
            nc.scalar.activation(
                out=capped[n][:, r, :],
                in_=score_banks[g][bank][:, col0 : col0 + width],
                func=ACT.Tanh,
                bias=kb_bias[:, r : r + 1],
                scale=1.0 / CAP,
            )

        def sigmoid(n, c0, width):
            prob[(n, c0)] = tile("prob%d_%d" % (n, c0), [P, PACK, width], F32)
            nc.scalar.activation(out=prob[(n, c0)][:], in_=capped[n][:, :, c0 : c0 + width], func=ACT.Sigmoid, scale=CAP)

        def weigh(n, c0, width):
            q0 = UNITS[n][2] + c0
            nc.vector.tensor_tensor(
                out=w_bf[n][:, c0 : c0 + width, :].rearrange("p (c i) r -> p c r i", i=2),
                in0=prob[(n, c0)][:].rearrange("p r (c i) -> p c r i", i=2),
                in1=mask_t[:, :, q0 : q0 + width].rearrange("p r (c i) -> p c r i", i=2),
                op=ALU.mult,
            )

        def quant_w(n, c0, width):
            cols = slice(c0, c0 + width)
            quantize(w_codes[n][:, cols], w_scales[n][:, cols], w_bf[n][:, cols, :].rearrange("p q r -> p (q r)"))

        def values(n):
            pair, g, q0, width = UNITS[n]
            bank, col0 = Y_PLACE[n]
            v_cols = slice(g * E, (g + 1) * E)
            for c in range(0, width, MM):
                product(
                    y_banks[bank][:, col0 + c : col0 + c + E],
                    w_codes[n][:, c : c + MM],
                    w_scales[n][:, c : c + MM],
                    v_codes[:, v_cols],
                    v_scales[:, v_cols],
                )

        def finish(first, last, on_scalar):
            pair, g, q0 = UNITS[first][:3]
            width = UNITS[last][2] + UNITS[last][3] - q0
            bank, col0 = Y_PLACE[first]
            head = PAIR_HEADS[pair][g]
            staged = y_sb[head][:, q0 // MM : (q0 + width) // MM, :]
            dst = staged.rearrange("p c e -> p (c e)")
            src = y_banks[bank][:, col0 : col0 + width]
            if on_scalar:
                nc.scalar.activation(out=dst, in_=src, func=ACT.Copy, scale=OUT_SCALE)
            else:
                nc.vector.tensor_scalar(out=dst, in0=src, scalar1=OUT_SCALE, scalar2=None, op0=ALU.mult)
            nc.sync.dma_start(out=out[head, q0 : q0 + width, :].rearrange("(c m) e -> m c e", m=MM), in_=staged)

        def each(step, places):
            for place in places:
                step(*place)

        def all_slots(*units):
            return [(n, r) for n in units for r in SLOTS]


        cast_k(nc.vector.tensor_copy, 0)
        nc.vector.tensor_scalar(out=kb_bias[:], in0=kb_sb[:], scalar1=1.0 / CAP, scalar2=None, op0=ALU.mult)
        cast_k(nc.scalar.copy, 1)
        cast_q(0, 0, 128)
        quant_k(0)
        quant_q(0, 0, 128)
        quant_k(1)
        opening = [(0, 0), (1, 0), (0, 1), (1, 1), (0, 2), (0, 3), (1, 2), (1, 3)]
        each(scores, opening)
        each(cap, opening)
        wide_pieces = [(0, 128), (128, 256)]
        each(cast_q, [(0, 128 + c0, width) for c0, width in wide_pieces])
        each(quant_q, [(0, 128 + c0, width) for c0, width in wide_pieces])
        scale_mask(0)
        sigmoid(0, 0, 128)
        load_second_pair_head(nc.scalar, 1)
        sigmoid(1, 0, 128)

        each(scores, [(2, 0), (2, 1), (3, 0), (2, 2)])
        weigh(0, 0, 128)
        for g in range(KV):
            cast_interleaved(v_bf[:, g], v_raw[:, g])
        weigh(1, 0, 128)
        quant_w(0, 0, 128)
        scale_mask(MASK_COLS)
        quant_w(1, 0, 128)
        quantize(v_codes[:], v_scales[:], v_bf[:].rearrange("p g e r -> p (g e r)"))
        cap(2, 0)
        each(scores, [(2, 3), (3, 1), (3, 2)])
        each(cap, [(2, 1), (3, 0)])
        scores(3, 3)
        each(cap, [(2, 2), (2, 3), (3, 1)])
        sigmoid(2, 0, 128)
        each(cap, [(3, 2), (3, 3)])
        each(sigmoid, [(2, 128, 256), (3, 0, 128), (3, 128, 256)])
        weigh(2, 0, 128)
        cast_q(1, 0, 256)
        quant_w(2, 0, 128)
        quant_q(1, 0, 256)
        weigh(2, 128, 256)
        weigh(3, 0, 128)
        cast_q(1, 256, 256)
        quant_w(3, 0, 128)
        quant_w(2, 128, 256)
        quant_q(1, 256, 256)

        each(scores, all_slots(4, 5))
        values(0)
        values(2)
        weigh(3, 128, 256)
        finish(0, 2, on_scalar=False)
        quant_w(3, 128, 256)
        each(cap, all_slots(4, 5)[:6])
        each(scores, all_slots(6, 7, 8))
        values(1)
        values(3)
        each(cap, all_slots(4, 5)[6:])
        each(sigmoid, [(4, 0, 256), (5, 0, 256)])
        each(weigh, [(4, 0, 256), (5, 0, 256)])
        quant_w(4, 0, 256)
        finish(1, 3, on_scalar=False)
        quant_w(5, 0, 256)
        values(4)
        values(5)

        each(cap, all_slots(6) + [(7, 0)])
        sigmoid(6, 0, 256)
        weigh(6, 0, 256)
        quant_w(6, 0, 256)
        values(6)
        halves = [(n, c0, 64) for n in (7, 8) for c0 in (0, 64)]
        each(cap, all_slots(7, 8)[1:6])
        sigmoid(*halves[0])
        each(cap, all_slots(7, 8)[6:])
        each(sigmoid, halves[1:])
        each(weigh, halves)
        quant_w(7, 0, 128)
        quant_w(8, 0, 128)

        finish(5, 5, on_scalar=True)
        finish(4, 6, on_scalar=True)
        values(7)
        values(8)
        finish(7, 7, on_scalar=False)
        finish(8, 8, on_scalar=True)
